import numpy as np
import ml_dtypes


def mxq(x, axis, fmt="e4m3"):
    dtype, down = {"e4m3": (ml_dtypes.float8_e4m3fn, 7), "e5m2": (ml_dtypes.float8_e5m2, 14)}[fmt]
    v = np.moveaxis(np.asarray(x, np.float32).astype(ml_dtypes.bfloat16).astype(np.float64), axis, -1)
    blocks = v.reshape(v.shape[:-1] + (-1, 32))
    amax = np.abs(blocks).max(-1, keepdims=True)
    byte = np.maximum(np.where(amax > 0, np.frexp(amax)[1] - 1 + 127, 0) - down, 1)
    scale = np.exp2(byte - 127.0)
    codes = (blocks / scale).astype(np.float32).astype(dtype).astype(np.float64)
    return np.moveaxis((codes * scale).reshape(v.shape), -1, axis)


WIDE = False


def mx_kscale(k):
    if not WIDE:
        return np.ones(k)
    levels = np.array([10, -10, 5, -5, 0])
    if k % 512:
        return np.exp2(np.random.permutation(np.resize(levels, k // 32))).repeat(32)
    a = np.empty((k // 512, 16))
    for p in range(k // 512):
        a[p, :8] = np.random.permutation(np.resize(levels, 8))
        for g in range(8):
            far = levels[np.abs(levels - a[p, g]) >= 10]
            a[p, g + 8] = far[np.random.randint(len(far))]
    return np.exp2(a.ravel()).repeat(32)


def f64(x):
    return np.asarray(x).astype(np.float64)


def striped(idx):
    return np.tile(idx.reshape(-1, 16).T, (8, 1)).astype(np.uint16)


def unstriped(offs):
    return offs[:16].T.reshape(-1).astype(np.int64)


def pack_weight(w):
    k, n = w.shape
    w = f64(np.asarray(w, np.float32).astype(ml_dtypes.bfloat16)).reshape(k // 32, 32, n)
    amax = np.abs(w).max(1)
    byte = np.clip(np.where(amax > 0, np.frexp(amax)[1] - 1 + 127 - 7, 1), 1, 254)
    scaled = (w * np.exp2(127.0 - byte)[:, None, :]).reshape(k, n).astype(np.float32)
    words = np.ascontiguousarray(scaled.reshape(k // 512, 128, 4, n).transpose(0, 1, 3, 2)).astype(ml_dtypes.float8_e4m3fn).view(np.uint8)
    return words, np.ascontiguousarray(byte.astype(np.uint8).reshape(k // 512, 16, n))


def unpack_weight(words, scales):
    g, p, n, _ = words.shape
    vals = np.ascontiguousarray(words).view(ml_dtypes.float8_e4m3fn).astype(np.float64) * np.repeat(np.exp2(scales.astype(np.float64) - 127.0), 8, axis=1)[..., None]
    return vals.transpose(0, 1, 3, 2).reshape(g * 512, n)


K, T, E, C, N = 1536, 1024, 8, 256, 256


def by_expert(wq, xq):
    return np.concatenate([wq[e].T @ xq[:, e * C:(e + 1) * C] for e in range(E)], axis=1)


def setup_inputs():
    n = np.random.standard_normal
    s = mx_kscale(K)[:, None]
    first = np.random.permutation(np.repeat(np.arange(E), T // E))
    second = (first + 1 + np.random.permutation(np.repeat(np.arange(E - 1), -(-T // (E - 1)))[:T])) % E
    while np.bincount(second, minlength=E).max() != T // E:
        load = np.bincount(second, minlength=E); hi, lo = int(load.argmax()), int(load.argmin())
        t = np.flatnonzero((second == hi) & (first != lo))[0]; second[t] = lo
    slot_token = np.empty(E * C, np.int64); pos = np.empty((2, T), np.int64); fill = np.zeros(E, np.int64)
    place = np.stack([np.random.permutation(C) for _ in range(E)])
    for r, deal in enumerate((first, second)):
        for t in np.random.permutation(T):
            e = deal[t]; j = e * C + place[e, fill[e]]; fill[e] += 1; slot_token[j] = t; pos[r, t] = j
    g = np.random.uniform(0.2, 0.8, T)
    packed = [pack_weight(m) for m in n((E, K, N)) / np.sqrt(K) / s[None]]
    return {
        "xT": (n((K, T)) * s).astype(np.float32),
        "w_words": np.stack([m[0] for m in packed]),
        "w_scales": np.stack([m[1] for m in packed]),
        "gate": np.stack([np.tile(g, (N, 1)), np.tile(1.0 - g, (N, 1))]).astype(np.float32),
        "offs": striped(slot_token),
        "pos1": striped(pos[0]),
        "pos2": striped(pos[1]),
    }


def reference(xT, w_words, w_scales, gate, offs, pos1, pos2):
    idx = unstriped(offs)
    xq = mxq(f64(xT)[:, idx], 0, "e4m3")
    w = np.stack([unpack_weight(w_words[e], w_scales[e]) for e in range(E)])
    y = by_expert(w, xq)
    return f64(gate[0]) * y[:, unstriped(pos1)] + f64(gate[1]) * y[:, unstriped(pos2)]

@@ -1,0 +1,205 @@
+from contextlib import ExitStack
+
+import concourse.mybir as mybir
+from concourse.masks import make_identity
+
+K, T, E, C, N = 1536, 1024, 8, 256, 256
+FLOPS = 2 * K * N * E * C
+
+F32 = mybir.dt.float32
+BF16 = mybir.dt.bfloat16
+I32 = mybir.dt.int32
+U32 = mybir.dt.uint32
+U16 = mybir.dt.uint16
+U8 = mybir.dt.uint8
+FP8X4 = mybir.dt.float8_e4m3fn_x4
+MULT = mybir.AluOpType.mult
+ADD = mybir.AluOpType.add
+
+P = 128
+PACK = 4
+PASSES = K // (P * PACK)
+SLOTS = E * C
+HALF = T // 2
+BANK = 512
+PIECES = ((0, 768), (768, 768), (1536, 512))
+
+
+def tile_routed_moe_kernel(tc, xT, w_words, w_scales, gate, offs, pos1, pos2, out):
+    nc = tc.nc
+    with ExitStack() as ctx:
+        keep = ctx.enter_context(tc.tile_pool(name="keep", bufs=1))
+        psum = ctx.enter_context(tc.psum_pool(name="psum", bufs=1))
+
+        offs_t = keep.tile([P, SLOTS // 16], U16, name="offs_t")
+        pos1_t = keep.tile([P, T // 16], U16, name="pos1_t")
+        pos2_t = keep.tile([P, T // 16], U16, name="pos2_t")
+
+        x_scales = keep.tile([P, T], U8, align_bytes=64, name="x_scales")
+        w_sc = keep.tile([P, E, N], U8, align_bytes=64, name="w_sc")
+        nc.gpsimd.memset(x_scales[:], 0)
+        nc.gpsimd.memset(w_sc[:], 0)
+        ident = keep.tile([P, P], F32, align_bytes=64, name="ident")
+        make_identity(nc, ident[:])
+
+        planes = xT.rearrange("(a p t) n -> a p t n", p=P, t=PACK)
+        raw = {}
+
+        def load(a, c0, width):
+            r = keep.tile([P, PACK, width], F32, align_bytes=64, name="raw%d_%d" % (a, c0))
+            nc.sync.dma_start(out=r[:], in_=planes[a, :, :, c0:c0 + width])
+            raw[a, c0] = (r, width)
+
+        for c0 in range(0, T, 256):
+            load(0, c0, 256)
+            if c0 == 0:
+                nc.sync.dma_start(offs_t[:], offs)
+        for a in range(1, PASSES):
+            for c0 in range(0, T, HALF):
+                load(a, c0, HALF)
+
+        for a in range(PASSES):
+            for q in range(4):
+                r0 = 32 * q + 4 * a
+                nc.sync.dma_start(
+                    out=w_sc[r0:r0 + 4, :, :].bitcast(I32),
+                    in_=w_scales[:, a, 4 * q:4 * q + 4, :].rearrange("e r n -> r e n").bitcast(I32),
+                )
+        w_t = []
+        for e in range(0, E, 2):
+            wt = keep.tile([P, 2 * PASSES, N], I32, align_bytes=64, name="w%d" % e)
+            nc.sync.dma_start(out=wt[:], in_=w_words[e:e + 2].rearrange("e a p n r -> p (e a) (n r)").bitcast(I32))
+            w_t.append(wt)
+        nc.sync.dma_start(pos1_t[:], pos1)
+        nc.sync.dma_start(pos2_t[:], pos2)
+        gates = {}
+        for nb in range(2):
+            for r in range(2):
+                gt = keep.tile([P, T], F32, align_bytes=64, name="gate%d_%d" % (nb, r))
+                nc.sync.dma_start(out=gt[:], in_=gate[r, nb * P:(nb + 1) * P, :])
+                gates[nb, r] = gt
+
+        x_words = [keep.tile([P, T], U32, align_bytes=64, name="x_words%d" % a) for a in range(PASSES)]
+        g_words = [keep.tile([P, SLOTS], U32, align_bytes=64, name="g_words%d" % a) for a in range(PASSES)]
+        g_scales = keep.tile([P, SLOTS], U8, align_bytes=64, name="g_scales")
+
+        def interleave(copy, a, c0):
+            r, width = raw[a, c0]
+            g = keep.tile([P, width, PACK], BF16, align_bytes=64, name="x16_%d_%d" % (a, c0))
+            copy(
+                out=g[:].rearrange("p (c i) t -> p c t i", i=4),
+                in_=r[:].rearrange("p t (c i) -> p c t i", i=4),
+            )
+            return g, width
+
+        def quantise(a, c0, gw):
+            g, width = gw
+            nc.vector.quantize_mx(
+                out=x_words[a][:, c0:c0 + width].bitcast(FP8X4),
+                scales=x_scales[4 * a:P, c0:c0 + width],
+                in_=g[:].rearrange("p w t -> p (w t)"),
+            )
+
+        def gather_words(a, s0, width):
+            nc.vector.tensor_copy(g_words[a][:, s0:s0 + width], x_words[a][:].indirect(offs_t[:, s0 // 16:(s0 + width) // 16]))
+
+        def gather_scales(s0, width):
+            nc.vector.tensor_copy(g_scales[:, s0:s0 + width], x_scales[:].indirect(offs_t[:, s0 // 16:(s0 + width) // 16]))
+
+        x16 = {}
+        for c0 in range(0, T, 256):
+            x16[0, c0] = interleave(nc.scalar.copy if c0 == 256 else nc.vector.tensor_copy, 0, c0)
+        for a in range(1, PASSES):
+            for c0 in range(0, T, HALF):
+                x16[a, c0] = interleave(nc.scalar.copy, a, c0)
+        for c0 in range(0, T, 256):
+            quantise(0, c0, x16[0, c0])
+        for a in range(PASSES):
+            if a > 0:
+                for c0 in range(0, T, HALF):
+                    quantise(a, c0, x16[a, c0])
+            if a < PASSES - 1:
+                for s0, width in PIECES:
+                    gather_words(a, s0, width)
+
+        y = [keep.tile([P, SLOTS], F32, align_bytes=64, name="y%d" % nb) for nb in range(2)]
+
+        def multiply(bank, half, nb, e):
+            cols = slice(e * C, (e + 1) * C)
+            for a in range(PASSES):
+                nc.tensor.matmul_mx(
+                    out=bank[:, half * C:(half + 1) * C],
+                    lhsT=w_t[e // 2][:, (e % 2) * PASSES + a, nb * P:(nb + 1) * P].bitcast(FP8X4),
+                    lhsT_scale=w_sc[4 * a:P, e, nb * P:(nb + 1) * P],
+                    rhs=g_words[a][:, cols].bitcast(FP8X4),
+                    rhs_scale=g_scales[4 * a:P, cols],
+                    start=(a == 0),
+                    stop=(a == PASSES - 1),
+                )
+
+        def new_bank(b):
+            return psum.tile([P, BANK], F32, tag="bank%d" % b, name="bank%d" % b)
+
+        def empty(bank, nb, e, count):
+            nc.scalar.copy(out=y[nb][:, e * C:(e + count) * C], in_=bank[:, 0:count * C])
+
+        last = PASSES - 1
+        gather_scales(0, 768)
+        gather_words(last, 0, 768)
+        gather_scales(768, 768)
+        gather_words(last, 768, 768)
+        gather_scales(1536, 512)
+        gather_words(last, 1536, C)
+        gather_words(last, 1792, C)
+
+        b00, b02, b04, b06, b07 = [new_bank(b) for b in range(5)]
+        b10, b12, b14 = [new_bank(b) for b in range(5, 8)]
+        multiply(b00, 0, 0, 0)
+        multiply(b00, 1, 0, 1)
+        empty(b00, 0, 0, 2)
+        multiply(b02, 0, 0, 2)
+        multiply(b10, 0, 1, 0)
+        multiply(b10, 1, 1, 1)
+        empty(b10, 1, 0, 2)
+        multiply(b12, 0, 1, 2)
+        multiply(b02, 1, 0, 3)
+        empty(b02, 0, 2, 2)
+        multiply(b04, 0, 0, 4)
+        multiply(b04, 1, 0, 5)
+        empty(b04, 0, 4, 2)
+        multiply(b06, 0, 0, 6)
+        empty(b06, 0, 6, 1)
+        multiply(b07, 0, 0, 7)
+        empty(b07, 0, 7, 1)
+        multiply(b12, 1, 1, 3)
+        empty(b12, 1, 2, 2)
+        multiply(b14, 0, 1, 4)
+        multiply(b14, 1, 1, 5)
+        empty(b14, 1, 4, 2)
+        b16 = new_bank(0)
+        multiply(b16, 0, 1, 6)
+        multiply(b16, 1, 1, 7)
+        empty(b16, 1, 6, 2)
+
+        first = keep.tile([P, T], F32, align_bytes=64, name="first0")
+        second = keep.tile([P, T], F32, align_bytes=64, name="second0")
+        total = keep.tile([P, T], F32, align_bytes=64, name="total0")
+        nc.vector.tensor_tensor(first[:], y[0][:].indirect(pos1_t[:]), gates[0, 0][:], MULT)
+        nc.vector.tensor_tensor(second[:], y[0][:].indirect(pos2_t[:]), gates[0, 1][:], MULT)
+        for h in range(2):
+            cols = slice(h * BANK, (h + 1) * BANK)
+            acc = new_bank(1 + h)
+            nc.tensor.matmul(acc[:], ident[:], first[:, cols], start=True, stop=False)
+            nc.tensor.matmul(acc[:], ident[:], second[:, cols], start=False, stop=True)
+            nc.scalar.copy(out=total[:, cols], in_=acc[:])
+            nc.sync.dma_start(out=out[0:P, cols], in_=total[:, cols])
+
+        first1 = keep.tile([P, T], F32, align_bytes=64, name="first1")
+        nc.vector.tensor_tensor(first1[:], y[1][:].indirect(pos1_t[:]), gates[1, 0][:], MULT)
+        for c0, width in ((0, 512), (512, 256), (768, 256)):
+            cols = slice(c0, c0 + width)
+            second1 = keep.tile([P, width], F32, align_bytes=64, name="second1_%d" % c0)
+            nc.vector.tensor_tensor(second1[:], y[1][:].indirect(pos2_t[:, c0 // 16:(c0 + width) // 16]), gates[1, 1][:, cols], MULT)
+            total1 = keep.tile([P, width], F32, align_bytes=64, name="total1_%d" % c0)
+            nc.vector.tensor_tensor(total1[:], first1[:, cols], second1[:], ADD)
+            nc.sync.dma_start(out=out[P:2 * P, cols], in_=total1[:])

@@ -50,10 +50,9 @@ def tile_routed_moe_kernel(tc, xT, w_words, w_scales, gate, offs, pos1, pos2, ou
             nc.sync.dma_start(out=r[:], in_=planes[a, :, :, c0:c0 + width])
             raw[a, c0] = (r, width)
 
-        for c0 in range(0, T, 256):
-            load(0, c0, 256)
-            if c0 == 0:
-                nc.sync.dma_start(offs_t[:], offs)
+        for c0, width in ((0, 512), (512, 256), (768, 256)):
+            load(0, c0, width)
+        nc.sync.dma_start(offs_t[:], offs)
         for a in range(1, PASSES):
             for c0 in range(0, T, HALF):
                 load(a, c0, HALF)
@@ -83,21 +82,22 @@ def tile_routed_moe_kernel(tc, xT, w_words, w_scales, gate, offs, pos1, pos2, ou
         g_words = [keep.tile([P, SLOTS], U32, align_bytes=64, name="g_words%d" % a) for a in range(PASSES)]
         g_scales = keep.tile([P, SLOTS], U8, align_bytes=64, name="g_scales")
 
-        def interleave(copy, a, c0):
-            r, width = raw[a, c0]
-            g = keep.tile([P, width, PACK], BF16, align_bytes=64, name="x16_%d_%d" % (a, c0))
-            copy(
-                out=g[:].rearrange("p (c i) t -> p c t i", i=4),
-                in_=r[:].rearrange("p t (c i) -> p c t i", i=4),
-            )
-            return g, width
+        x16 = {}
 
-        def quantise(a, c0, gw):
-            g, width = gw
+        def interleave(copy, a, c0, lo, hi):
+            r, width = raw[a, c0]
+            if (a, c0) not in x16:
+                x16[a, c0] = keep.tile([P, width, PACK], BF16, align_bytes=64, name="x16_%d_%d" % (a, c0))
+            copy(
+                out=x16[a, c0][:, lo:hi, :].rearrange("p (c i) t -> p c t i", i=4),
+                in_=r[:, :, lo:hi].rearrange("p t (c i) -> p c t i", i=4),
+            )
+
+        def quantise(a, c0, lo, hi):
             nc.vector.quantize_mx(
-                out=x_words[a][:, c0:c0 + width].bitcast(FP8X4),
-                scales=x_scales[4 * a:P, c0:c0 + width],
-                in_=g[:].rearrange("p w t -> p (w t)"),
+                out=x_words[a][:, c0 + lo:c0 + hi].bitcast(FP8X4),
+                scales=x_scales[4 * a:P, c0 + lo:c0 + hi],
+                in_=x16[a, c0][:, lo:hi, :].rearrange("p w t -> p (w t)"),
             )
 
         def gather_words(a, s0, width):
@@ -106,18 +106,23 @@ def tile_routed_moe_kernel(tc, xT, w_words, w_scales, gate, offs, pos1, pos2, ou
         def gather_scales(s0, width):
             nc.vector.tensor_copy(g_scales[:, s0:s0 + width], x_scales[:].indirect(offs_t[:, s0 // 16:(s0 + width) // 16]))
 
-        x16 = {}
-        for c0 in range(0, T, 256):
-            x16[0, c0] = interleave(nc.scalar.copy if c0 == 256 else nc.vector.tensor_copy, 0, c0)
+        vec, sca, gps = nc.vector.tensor_copy, nc.scalar.copy, nc.gpsimd.tensor_copy
+        interleave(sca, 0, 0, 256, 512)
+        interleave(vec, 0, 0, 0, 256)
+        interleave(vec, 0, 512, 0, 256)
+        quantise(0, 0, 0, 512)
+        interleave(sca, 0, 768, 128, 256)
+        interleave(vec, 0, 768, 0, 128)
+        quantise(0, 512, 0, 256)
+        quantise(0, 768, 0, 256)
         for a in range(1, PASSES):
-            for c0 in range(0, T, HALF):
-                x16[a, c0] = interleave(nc.scalar.copy, a, c0)
-        for c0 in range(0, T, 256):
-            quantise(0, c0, x16[0, c0])
+            interleave(gps, a, 0, 0, 256)
+            interleave(sca, a, 0, 256, 512)
+            interleave(sca, a, 512, 0, 512)
         for a in range(PASSES):
             if a > 0:
                 for c0 in range(0, T, HALF):
-                    quantise(a, c0, x16[a, c0])
+                    quantise(a, c0, 0, 512)
             if a < PASSES - 1:
                 for s0, width in PIECES:
                     gather_words(a, s0, width)
@@ -196,10 +201,19 @@ def tile_routed_moe_kernel(tc, xT, w_words, w_scales, gate, offs, pos1, pos2, ou
 
         first1 = keep.tile([P, T], F32, align_bytes=64, name="first1")
         nc.vector.tensor_tensor(first1[:], y[1][:].indirect(pos1_t[:]), gates[1, 0][:], MULT)
-        for c0, width in ((0, 512), (512, 256), (768, 256)):
+        second1 = {}
+        for c0, width in ((0, 256), (256, 512), (768, 256)):
             cols = slice(c0, c0 + width)
-            second1 = keep.tile([P, width], F32, align_bytes=64, name="second1_%d" % c0)
-            nc.vector.tensor_tensor(second1[:], y[1][:].indirect(pos2_t[:, c0 // 16:(c0 + width) // 16]), gates[1, 1][:, cols], MULT)
-            total1 = keep.tile([P, width], F32, align_bytes=64, name="total1_%d" % c0)
-            nc.vector.tensor_tensor(total1[:], first1[:, cols], second1[:], ADD)
-            nc.sync.dma_start(out=out[P:2 * P, cols], in_=total1[:])
+            second1[c0] = keep.tile([P, width], F32, align_bytes=64, name="second1_%d" % c0)
+            nc.vector.tensor_tensor(second1[c0][:], y[1][:].indirect(pos2_t[:, c0 // 16:(c0 + width) // 16]), gates[1, 1][:, cols], MULT)
+        total1 = keep.tile([P, 256], F32, align_bytes=64, name="total1_0")
+        acc = new_bank(3)
+        nc.tensor.matmul(acc[:, 0:256], ident[:], first1[:, 0:256], start=True, stop=False)
+        nc.tensor.matmul(acc[:, 0:256], ident[:], second1[0][:], start=False, stop=True)
+        nc.scalar.copy(out=total1[:], in_=acc[:, 0:256])
+        nc.sync.dma_start(out=out[P:2 * P, 0:256], in_=total1[:])
+        for c0, width in ((256, 512), (768, 256)):
+            cols = slice(c0, c0 + width)
+            tail = keep.tile([P, width], F32, align_bytes=64, name="total1_%d" % c0)
+            nc.vector.tensor_tensor(tail[:], first1[:, cols], second1[c0][:], ADD)
+            nc.sync.dma_start(out=out[P:2 * P, cols], in_=tail[:])

@@ -38,7 +38,7 @@ def tile_routed_moe_kernel(tc, xT, w_words, w_scales, gate, offs, pos1, pos2, ou
         x_scales = keep.tile([P, T], U8, align_bytes=64, name="x_scales")
         w_sc = keep.tile([P, E, N], U8, align_bytes=64, name="w_sc")
         nc.gpsimd.memset(x_scales[:], 0)
-        nc.gpsimd.memset(w_sc[:], 0)
+        nc.vector.memset(w_sc[:].rearrange("p e n -> p (e n)").bitcast(I32), 0)
         ident = keep.tile([P, P], F32, align_bytes=64, name="ident")
         make_identity(nc, ident[:])
 
@@ -106,7 +106,7 @@ def tile_routed_moe_kernel(tc, xT, w_words, w_scales, gate, offs, pos1, pos2, ou
         def gather_scales(s0, width):
             nc.vector.tensor_copy(g_scales[:, s0:s0 + width], x_scales[:].indirect(offs_t[:, s0 // 16:(s0 + width) // 16]))
 
-        vec, sca, gps = nc.vector.tensor_copy, nc.scalar.copy, nc.gpsimd.tensor_copy
+        vec, sca = nc.vector.tensor_copy, nc.scalar.copy
         interleave(sca, 0, 0, 256, 512)
         interleave(vec, 0, 0, 0, 256)
         interleave(vec, 0, 512, 0, 256)
@@ -116,8 +116,7 @@ def tile_routed_moe_kernel(tc, xT, w_words, w_scales, gate, offs, pos1, pos2, ou
         quantise(0, 512, 0, 256)
         quantise(0, 768, 0, 256)
         for a in range(1, PASSES):
-            interleave(gps, a, 0, 0, 256)
-            interleave(sca, a, 0, 256, 512)
+            interleave(sca, a, 0, 0, 512)
             interleave(sca, a, 512, 0, 512)
         for a in range(PASSES):
             if a > 0:
@@ -187,33 +186,37 @@ def tile_routed_moe_kernel(tc, xT, w_words, w_scales, gate, offs, pos1, pos2, ou
         empty(b16, 1, 6, 2)
 
         first = keep.tile([P, T], F32, align_bytes=64, name="first0")
-        second = keep.tile([P, T], F32, align_bytes=64, name="second0")
+        second0 = keep.tile([P, T], F32, align_bytes=64, name="second0")
         total = keep.tile([P, T], F32, align_bytes=64, name="total0")
         nc.vector.tensor_tensor(first[:], y[0][:].indirect(pos1_t[:]), gates[0, 0][:], MULT)
-        nc.vector.tensor_tensor(second[:], y[0][:].indirect(pos2_t[:]), gates[0, 1][:], MULT)
+        halves = [slice(h * BANK, (h + 1) * BANK) for h in range(2)]
+        accs = [new_bank(1 + h) for h in range(2)]
         for h in range(2):
-            cols = slice(h * BANK, (h + 1) * BANK)
-            acc = new_bank(1 + h)
-            nc.tensor.matmul(acc[:], ident[:], first[:, cols], start=True, stop=False)
-            nc.tensor.matmul(acc[:], ident[:], second[:, cols], start=False, stop=True)
-            nc.scalar.copy(out=total[:, cols], in_=acc[:])
-            nc.sync.dma_start(out=out[0:P, cols], in_=total[:, cols])
+            nc.vector.tensor_tensor(second0[:, halves[h]], y[0][:].indirect(pos2_t[:, h * BANK // 16:(h + 1) * BANK // 16]), gates[0, 1][:, halves[h]], MULT)
+        for h in range(2):
+            nc.tensor.matmul(accs[h][:], ident[:], first[:, halves[h]], start=True, stop=False)
+        for h in range(2):
+            nc.tensor.matmul(accs[h][:], ident[:], second0[:, halves[h]], start=False, stop=True)
+            nc.scalar.copy(out=total[:, halves[h]], in_=accs[h][:])
+            nc.scalar.dma_start(out=out[0:P, halves[h]], in_=total[:, halves[h]])
 
         first1 = keep.tile([P, T], F32, align_bytes=64, name="first1")
         nc.vector.tensor_tensor(first1[:], y[1][:].indirect(pos1_t[:]), gates[1, 0][:], MULT)
-        second1 = {}
-        for c0, width in ((0, 256), (256, 512), (768, 256)):
-            cols = slice(c0, c0 + width)
+        second1, total1 = {}, {}
+
+        def second(c0, width):
             second1[c0] = keep.tile([P, width], F32, align_bytes=64, name="second1_%d" % c0)
-            nc.vector.tensor_tensor(second1[c0][:], y[1][:].indirect(pos2_t[:, c0 // 16:(c0 + width) // 16]), gates[1, 1][:, cols], MULT)
-        total1 = keep.tile([P, 256], F32, align_bytes=64, name="total1_0")
-        acc = new_bank(3)
-        nc.tensor.matmul(acc[:, 0:256], ident[:], first1[:, 0:256], start=True, stop=False)
-        nc.tensor.matmul(acc[:, 0:256], ident[:], second1[0][:], start=False, stop=True)
-        nc.scalar.copy(out=total1[:], in_=acc[:, 0:256])
-        nc.sync.dma_start(out=out[P:2 * P, 0:256], in_=total1[:])
-        for c0, width in ((256, 512), (768, 256)):
+            nc.vector.tensor_tensor(second1[c0][:], y[1][:].indirect(pos2_t[:, c0 // 16:(c0 + width) // 16]), gates[1, 1][:, c0:c0 + width], MULT)
+
+        def add(c0, width):
             cols = slice(c0, c0 + width)
-            tail = keep.tile([P, width], F32, align_bytes=64, name="total1_%d" % c0)
-            nc.vector.tensor_tensor(tail[:], first1[:, cols], second1[c0][:], ADD)
-            nc.sync.dma_start(out=out[P:2 * P, cols], in_=tail[:])
+            total1[c0] = keep.tile([P, width], F32, align_bytes=64, name="total1_%d" % c0)
+            nc.vector.tensor_tensor(total1[c0][:], first1[:, cols], second1[c0][:], ADD)
+            nc.sync.dma_start(out=out[P:2 * P, cols], in_=total1[c0][:])
+
+        second(0, 512)
+        second(512, 256)
+        add(0, 512)
+        second(768, 256)
+        add(512, 256)
+        add(768, 256)

@@ -53,9 +53,9 @@ def tile_routed_moe_kernel(tc, xT, w_words, w_scales, gate, offs, pos1, pos2, ou
         for c0, width in ((0, 512), (512, 256), (768, 256)):
             load(0, c0, width)
         nc.sync.dma_start(offs_t[:], offs)
-        for a in range(1, PASSES):
-            for c0 in range(0, T, HALF):
-                load(a, c0, HALF)
+        for a, width in ((1, 256), (2, HALF)):
+            for c0 in range(0, T, width):
+                load(a, c0, width)
 
         for a in range(PASSES):
             for q in range(4):
@@ -84,12 +84,14 @@ def tile_routed_moe_kernel(tc, xT, w_words, w_scales, gate, offs, pos1, pos2, ou
 
         x16 = {}
 
-        def interleave(copy, a, c0, lo, hi):
+        def interleave(copy, a, c0, lo, hi, base=None):
+            base = c0 if base is None else base
             r, width = raw[a, c0]
-            if (a, c0) not in x16:
-                x16[a, c0] = keep.tile([P, width, PACK], BF16, align_bytes=64, name="x16_%d_%d" % (a, c0))
+            if (a, base) not in x16:
+                x16[a, base] = keep.tile([P, HALF, PACK], BF16, align_bytes=64, name="x16_%d_%d" % (a, base))
+            at = c0 - base
             copy(
-                out=x16[a, c0][:, lo:hi, :].rearrange("p (c i) t -> p c t i", i=4),
+                out=x16[a, base][:, at + lo:at + hi, :].rearrange("p (c i) t -> p c t i", i=4),
                 in_=r[:, :, lo:hi].rearrange("p t (c i) -> p c t i", i=4),
             )
 
@@ -115,9 +117,10 @@ def tile_routed_moe_kernel(tc, xT, w_words, w_scales, gate, offs, pos1, pos2, ou
         interleave(vec, 0, 768, 0, 128)
         quantise(0, 512, 0, 256)
         quantise(0, 768, 0, 256)
-        for a in range(1, PASSES):
-            interleave(sca, a, 0, 0, 512)
-            interleave(sca, a, 512, 0, 512)
+        for c0 in range(0, T, 256):
+            interleave(sca, 1, c0, 0, 256, c0 // HALF * HALF)
+        for c0 in range(0, T, HALF):
+            interleave(sca, 2, c0, 0, HALF)
         for a in range(PASSES):
             if a > 0:
                 for c0 in range(0, T, HALF):

from contextlib import ExitStack

import concourse.mybir as mybir
from concourse.masks import make_identity

K, T, E, C, N = 1536, 1024, 8, 256, 256
FLOPS = 2 * K * N * E * C

F32 = mybir.dt.float32
BF16 = mybir.dt.bfloat16
I32 = mybir.dt.int32
U32 = mybir.dt.uint32
U16 = mybir.dt.uint16
U8 = mybir.dt.uint8
FP8X4 = mybir.dt.float8_e4m3fn_x4
MULT = mybir.AluOpType.mult
ADD = mybir.AluOpType.add

P = 128
PACK = 4
PASSES = K // (P * PACK)
SLOTS = E * C
HALF = T // 2
BANK = 512
PIECES = ((0, 768), (768, 768), (1536, 512))


def tile_routed_moe_kernel(tc, xT, w_words, w_scales, gate, offs, pos1, pos2, out):
    nc = tc.nc
    with ExitStack() as ctx:
        keep = ctx.enter_context(tc.tile_pool(name="keep", bufs=1))
        psum = ctx.enter_context(tc.psum_pool(name="psum", bufs=1))

        offs_t = keep.tile([P, SLOTS // 16], U16, name="offs_t")
        pos1_t = keep.tile([P, T // 16], U16, name="pos1_t")
        pos2_t = keep.tile([P, T // 16], U16, name="pos2_t")

        x_scales = keep.tile([P, T], U8, align_bytes=64, name="x_scales")
        w_sc = keep.tile([P, E, N], U8, align_bytes=64, name="w_sc")
        nc.gpsimd.memset(x_scales[:], 0)
        nc.vector.memset(w_sc[:].rearrange("p e n -> p (e n)").bitcast(I32), 0)
        ident = keep.tile([P, P], F32, align_bytes=64, name="ident")
        make_identity(nc, ident[:])

        planes = xT.rearrange("(a p t) n -> a p t n", p=P, t=PACK)
        raw = {}

        def load(a, c0, width):
            r = keep.tile([P, PACK, width], F32, align_bytes=64, name="raw%d_%d" % (a, c0))
            nc.sync.dma_start(out=r[:], in_=planes[a, :, :, c0:c0 + width])
            raw[a, c0] = (r, width)

        for c0, width in ((0, 512), (512, 256), (768, 256)):
            load(0, c0, width)
        nc.sync.dma_start(offs_t[:], offs)
        for a, width in ((1, 256), (2, HALF)):
            for c0 in range(0, T, width):
                load(a, c0, width)

        for a in range(PASSES):
            for q in range(4):
                r0 = 32 * q + 4 * a
                nc.sync.dma_start(
                    out=w_sc[r0:r0 + 4, :, :].bitcast(I32),
                    in_=w_scales[:, a, 4 * q:4 * q + 4, :].rearrange("e r n -> r e n").bitcast(I32),
                )
        w_t = []
        for e in range(0, E, 2):
            wt = keep.tile([P, 2 * PASSES, N], I32, align_bytes=64, name="w%d" % e)
            nc.sync.dma_start(out=wt[:], in_=w_words[e:e + 2].rearrange("e a p n r -> p (e a) (n r)").bitcast(I32))
            w_t.append(wt)
        nc.sync.dma_start(pos1_t[:], pos1)
        nc.sync.dma_start(pos2_t[:], pos2)
        gates = {}
        for nb in range(2):
            for r in range(2):
                gt = keep.tile([P, T], F32, align_bytes=64, name="gate%d_%d" % (nb, r))
                nc.sync.dma_start(out=gt[:], in_=gate[r, nb * P:(nb + 1) * P, :])
                gates[nb, r] = gt

        x_words = [keep.tile([P, T], U32, align_bytes=64, name="x_words%d" % a) for a in range(PASSES)]
        g_words = [keep.tile([P, SLOTS], U32, align_bytes=64, name="g_words%d" % a) for a in range(PASSES)]
        g_scales = keep.tile([P, SLOTS], U8, align_bytes=64, name="g_scales")

        x16 = {}

        def interleave(copy, a, c0, lo, hi, base=None):
            base = c0 if base is None else base
            r, width = raw[a, c0]
            if (a, base) not in x16:
                x16[a, base] = keep.tile([P, HALF, PACK], BF16, align_bytes=64, name="x16_%d_%d" % (a, base))
            at = c0 - base
            copy(
                out=x16[a, base][:, at + lo:at + hi, :].rearrange("p (c i) t -> p c t i", i=4),
                in_=r[:, :, lo:hi].rearrange("p t (c i) -> p c t i", i=4),
            )

        def quantise(a, c0, lo, hi):
            nc.vector.quantize_mx(
                out=x_words[a][:, c0 + lo:c0 + hi].bitcast(FP8X4),
                scales=x_scales[4 * a:P, c0 + lo:c0 + hi],
                in_=x16[a, c0][:, lo:hi, :].rearrange("p w t -> p (w t)"),
            )

        def gather_words(a, s0, width):
            nc.vector.tensor_copy(g_words[a][:, s0:s0 + width], x_words[a][:].indirect(offs_t[:, s0 // 16:(s0 + width) // 16]))

        def gather_scales(s0, width):
            nc.vector.tensor_copy(g_scales[:, s0:s0 + width], x_scales[:].indirect(offs_t[:, s0 // 16:(s0 + width) // 16]))

        vec, sca = nc.vector.tensor_copy, nc.scalar.copy
        interleave(sca, 0, 0, 256, 512)
        interleave(vec, 0, 0, 0, 256)
        interleave(vec, 0, 512, 0, 256)
        quantise(0, 0, 0, 512)
        interleave(sca, 0, 768, 128, 256)
        interleave(vec, 0, 768, 0, 128)
        quantise(0, 512, 0, 256)
        quantise(0, 768, 0, 256)
        for c0 in range(0, T, 256):
            interleave(sca, 1, c0, 0, 256, c0 // HALF * HALF)
        for c0 in range(0, T, HALF):
            interleave(sca, 2, c0, 0, HALF)
        for a in range(PASSES):
            if a > 0:
                for c0 in range(0, T, HALF):
                    quantise(a, c0, 0, 512)
            if a < PASSES - 1:
                for s0, width in PIECES:
                    gather_words(a, s0, width)

        y = [keep.tile([P, SLOTS], F32, align_bytes=64, name="y%d" % nb) for nb in range(2)]

        def multiply(bank, half, nb, e):
            cols = slice(e * C, (e + 1) * C)
            for a in range(PASSES):
                nc.tensor.matmul_mx(
                    out=bank[:, half * C:(half + 1) * C],
                    lhsT=w_t[e // 2][:, (e % 2) * PASSES + a, nb * P:(nb + 1) * P].bitcast(FP8X4),
                    lhsT_scale=w_sc[4 * a:P, e, nb * P:(nb + 1) * P],
                    rhs=g_words[a][:, cols].bitcast(FP8X4),
                    rhs_scale=g_scales[4 * a:P, cols],
                    start=(a == 0),
                    stop=(a == PASSES - 1),
                )

        def new_bank(b):
            return psum.tile([P, BANK], F32, tag="bank%d" % b, name="bank%d" % b)

        def empty(bank, nb, e, count):
            nc.scalar.copy(out=y[nb][:, e * C:(e + count) * C], in_=bank[:, 0:count * C])

        last = PASSES - 1
        gather_scales(0, 768)
        gather_words(last, 0, 768)
        gather_scales(768, 768)
        gather_words(last, 768, 768)
        gather_scales(1536, 512)
        gather_words(last, 1536, C)
        gather_words(last, 1792, C)

        b00, b02, b04, b06, b07 = [new_bank(b) for b in range(5)]
        b10, b12, b14 = [new_bank(b) for b in range(5, 8)]
        multiply(b00, 0, 0, 0)
        multiply(b00, 1, 0, 1)
        empty(b00, 0, 0, 2)
        multiply(b02, 0, 0, 2)
        multiply(b10, 0, 1, 0)
        multiply(b10, 1, 1, 1)
        empty(b10, 1, 0, 2)
        multiply(b12, 0, 1, 2)
        multiply(b02, 1, 0, 3)
        empty(b02, 0, 2, 2)
        multiply(b04, 0, 0, 4)
        multiply(b04, 1, 0, 5)
        empty(b04, 0, 4, 2)
        multiply(b06, 0, 0, 6)
        empty(b06, 0, 6, 1)
        multiply(b07, 0, 0, 7)
        empty(b07, 0, 7, 1)
        multiply(b12, 1, 1, 3)
        empty(b12, 1, 2, 2)
        multiply(b14, 0, 1, 4)
        multiply(b14, 1, 1, 5)
        empty(b14, 1, 4, 2)
        b16 = new_bank(0)
        multiply(b16, 0, 1, 6)
        multiply(b16, 1, 1, 7)
        empty(b16, 1, 6, 2)

        first = keep.tile([P, T], F32, align_bytes=64, name="first0")
        second0 = keep.tile([P, T], F32, align_bytes=64, name="second0")
        total = keep.tile([P, T], F32, align_bytes=64, name="total0")
        nc.vector.tensor_tensor(first[:], y[0][:].indirect(pos1_t[:]), gates[0, 0][:], MULT)
        halves = [slice(h * BANK, (h + 1) * BANK) for h in range(2)]
        accs = [new_bank(1 + h) for h in range(2)]
        for h in range(2):
            nc.vector.tensor_tensor(second0[:, halves[h]], y[0][:].indirect(pos2_t[:, h * BANK // 16:(h + 1) * BANK // 16]), gates[0, 1][:, halves[h]], MULT)
        for h in range(2):
            nc.tensor.matmul(accs[h][:], ident[:], first[:, halves[h]], start=True, stop=False)
        for h in range(2):
            nc.tensor.matmul(accs[h][:], ident[:], second0[:, halves[h]], start=False, stop=True)
            nc.scalar.copy(out=total[:, halves[h]], in_=accs[h][:])
            nc.scalar.dma_start(out=out[0:P, halves[h]], in_=total[:, halves[h]])

        first1 = keep.tile([P, T], F32, align_bytes=64, name="first1")
        nc.vector.tensor_tensor(first1[:], y[1][:].indirect(pos1_t[:]), gates[1, 0][:], MULT)
        second1, total1 = {}, {}

        def second(c0, width):
            second1[c0] = keep.tile([P, width], F32, align_bytes=64, name="second1_%d" % c0)
            nc.vector.tensor_tensor(second1[c0][:], y[1][:].indirect(pos2_t[:, c0 // 16:(c0 + width) // 16]), gates[1, 1][:, c0:c0 + width], MULT)

        def add(c0, width):
            cols = slice(c0, c0 + width)
            total1[c0] = keep.tile([P, width], F32, align_bytes=64, name="total1_%d" % c0)
            nc.vector.tensor_tensor(total1[c0][:], first1[:, cols], second1[c0][:], ADD)
            nc.sync.dma_start(out=out[P:2 * P, cols], in_=total1[c0][:])

        second(0, 512)
        second(512, 256)
        add(0, 512)
        second(768, 256)
        add(512, 256)
        add(768, 256)
